import numpy as np
import ml_dtypes


def mxq(x, axis, fmt="e4m3"):
    dtype, down = {"e4m3": (ml_dtypes.float8_e4m3fn, 7), "e5m2": (ml_dtypes.float8_e5m2, 14)}[fmt]
    v = np.moveaxis(np.asarray(x, np.float32).astype(ml_dtypes.bfloat16).astype(np.float64), axis, -1)
    blocks = v.reshape(v.shape[:-1] + (-1, 32))
    amax = np.abs(blocks).max(-1, keepdims=True)
    byte = np.maximum(np.where(amax > 0, np.frexp(amax)[1] - 1 + 127, 0) - down, 1)
    scale = np.exp2(byte - 127.0)
    codes = (blocks / scale).astype(np.float32).astype(dtype).astype(np.float64)
    return np.moveaxis((codes * scale).reshape(v.shape), -1, axis)


WIDE = False


def mx_kscale(k):
    if not WIDE:
        return np.ones(k)
    levels = np.array([30, -30])
    if k % 512:
        return np.exp2(np.random.permutation(np.resize(levels, k // 32))).repeat(32)
    a = np.empty((k // 512, 16))
    for p in range(k // 512):
        a[p, :8] = np.random.permutation(np.resize(levels, 8))
        for g in range(8):
            far = levels[np.abs(levels - a[p, g]) >= 10]
            a[p, g + 8] = far[np.random.randint(len(far))]
    return np.exp2(a.ravel()).repeat(32)


def f64(x):
    return np.asarray(x).astype(np.float64)


def striped(idx):
    return np.tile(idx.reshape(-1, 16).T, (8, 1)).astype(np.uint16)


def unstriped(offs):
    return offs[:16].T.reshape(-1).astype(np.int64)


def d_relu2(v):
    return 2.0 * np.maximum(v, 0.0)


K, T, E, C, H, N = 384, 2048, 4, 512, 1024, 512


def by_expert(wq, xq):
    return np.concatenate([wq[e].T @ xq[:, e * C:(e + 1) * C] for e in range(E)], axis=1)


def setup_inputs():
    n = np.random.standard_normal
    s = mx_kscale(N)[:, None]
    u = mx_kscale(H)
    return {
        "dyT": (n((N, T)) * s).astype(np.float32),
        "a": n((H, E * C)).astype(np.float32),
        "w2": (n((E, N, H)) / np.sqrt(N) / s[None] * u[None, None, :]).astype(np.float32),
        "w1": (n((E, H, K)) / np.sqrt(H) / u[None, :, None]).astype(np.float32),
        "gate": np.tile(np.random.uniform(0.2, 1.0, E * C), (N, 1)).astype(np.float32),
        "offs": striped(np.random.permutation(T)[:E * C]),
    }


def reference(dyT, a, w2, w1, gate, offs):
    idx = unstriped(offs)
    gq = mxq(f64(gate) * f64(dyT)[:, idx], 0, "e5m2")
    dh = by_expert(mxq(f64(w2), 1, "e4m3"), gq)
    da = dh * d_relu2(f64(a))
    dx = by_expert(mxq(f64(w1), 1, "e4m3"), mxq(da, 0, "e5m2"))
    out = np.zeros((K, T))
    out[:, idx] = dx
    return out

@@ -1,0 +1,164 @@
+from contextlib import ExitStack
+
+import concourse.mybir as mybir
+
+K, T, E, C, H, N = 384, 2048, 4, 512, 1024, 512
+P = 128
+J = 4
+HALVES = H // (P * J)
+K_TILES = K // P
+FLOPS = 2 * E * C * (N * H + H * K)
+BYTES = 4 * (N * T + H * E * C + E * N * H + E * H * K + E * C + K * T) + 2 * P * (E * C // 16)
+
+F32 = mybir.dt.float32
+BF16 = mybir.dt.bfloat16
+U32 = mybir.dt.uint32
+U16 = mybir.dt.uint16
+U8 = mybir.dt.uint8
+E4M3 = mybir.dt.float8_e4m3fn_x4
+E5M2 = mybir.dt.float8_e5m2_x4
+MULT = mybir.AluOpType.mult
+MAX = mybir.AluOpType.max
+COPY = mybir.ActivationFunctionType.Copy
+
+
+def tile_moe_bdx_mlp_relu2_kernel(tc, dyT, a, w2, w1, gate, offs, out):
+    nc = tc.nc
+    with ExitStack() as ctx:
+        held = ctx.enter_context(tc.tile_pool(name="held", bufs=1))
+        work = ctx.enter_context(tc.tile_pool(name="work", bufs=2))
+        psum = ctx.enter_context(tc.psum_pool(name="psum", bufs=1))
+
+        offsets = held.tile([P, E * C // 16], U16, name="offsets")
+        nc.sync.dma_start(offsets[:], offs)
+        gates = [held.tile([P, C], F32, name=f"gate{e}") for e in range(E)]
+        tokens = [held.tile([P, T], F32, name=f"tokens{t}") for t in range(J)]
+        windows = [held.tile([P, T], F32, name=f"window{k}") for k in range(K_TILES)]
+
+        def load_gate(e):
+            nc.sync.dma_start(gates[e][:], gate[0:P, e * C : (e + 1) * C])
+
+        dy_rows = dyT.rearrange("(p t) s -> p t s", t=J)
+        load_gate(0)
+        nc.sync.dma_start(tokens[0][:], dy_rows[:, 0, :])
+        load_gate(1)
+        for t in range(1, J):
+            nc.sync.dma_start(tokens[t][:], dy_rows[:, t, :])
+
+        a_rows = a.rearrange("(h p t) s -> h p t s", p=P, t=J)
+        results = []
+        for e in range(E):
+            slots = slice(e * C, (e + 1) * C)
+            w2_rows = w2[e].rearrange("(p j) i -> p j i", j=J)
+            w1_rows = w1[e].rearrange("(h p j) k -> h p j k", p=P, j=J)
+
+            w2_raw = []
+            for h in range(HALVES):
+                raw = work.tile([P, J, P * J], F32, name="w2_raw", bufs=3)
+                nc.sync.dma_start(raw[:], w2_rows[:, :, h * P * J : (h + 1) * P * J])
+                w2_raw.append(raw)
+            if e == 0:
+                load_gate(2)
+                load_gate(3)
+            a_raw = []
+            for h in range(HALVES):
+                raw = work.tile([P, J, C], F32, name="a_raw", bufs=3)
+                nc.sync.dma_start(raw[:], a_rows[h][:, :, slots])
+                a_raw.append(raw)
+            w1_raw = []
+            for h in range(HALVES):
+                raw = work.tile([P, J, K], F32, name="w1_raw", bufs=2)
+                nc.sync.dma_start(raw[:], w1_rows[h])
+                w1_raw.append(raw)
+
+            gathered = work.tile([P, J, C], F32, name="gathered")
+            for t in range(J):
+                nc.vector.tensor_tensor(
+                    gathered[:, t, :], tokens[t][:].indirect(offsets[:, e * C // 16 : (e + 1) * C // 16]), gates[e][:], MULT
+                )
+            g_bf = work.tile([P, C, J], BF16, name="g_bf", align_bytes=64)
+            nc.scalar.activation(
+                g_bf[:].rearrange("p (c i) t -> p c t i", i=4), gathered[:].rearrange("p t (c i) -> p c t i", i=4), COPY
+            )
+            g_codes = work.tile([P, C], U32, name="g_codes", align_bytes=64)
+            g_scales = work.tile([P, C], U8, name="g_scales", align_bytes=64)
+            nc.vector.quantize_mx(
+                out=g_codes[:].bitcast(E5M2), scales=g_scales[:], in_=g_bf[:].rearrange("p c t -> p (c t)")
+            )
+
+            w2_codes = work.tile([P, H], U32, name="w2_codes", align_bytes=64)
+            w2_scales = work.tile([P, H], U8, name="w2_scales", align_bytes=64)
+            for h in range(HALVES):
+                w2_bf = work.tile([P, J, P, J], BF16, name="w2_bf", align_bytes=64)
+                nc.scalar.activation(
+                    w2_bf[:].rearrange("p t m j -> p m t j"), w2_raw[h][:].rearrange("p j (m t) -> p m t j", t=J), COPY
+                )
+                cols = slice(h * P * J, (h + 1) * P * J)
+                nc.vector.quantize_mx(
+                    out=w2_codes[:, cols].bitcast(E4M3), scales=w2_scales[:, cols], in_=w2_bf[:].rearrange("p t m j -> p (t m j)")
+                )
+
+            w1_bf = work.tile([P, HALVES * K, J], BF16, name="w1_bf", align_bytes=64)
+            w1_codes = work.tile([P, HALVES * K], U32, name="w1_codes", align_bytes=64)
+            w1_scales = work.tile([P, HALVES * K], U8, name="w1_scales", align_bytes=64)
+            da_codes = []
+            for h in range(HALVES):
+                da_bf = work.tile([P, J, C], BF16, name="da_bf")
+                for t in range(J):
+                    dh = psum.tile([P, C], F32, name="dh", bufs=5)
+                    col = (h * J + t) * P
+                    nc.tensor.matmul_mx(
+                        out=dh[:],
+                        lhsT=w2_codes[:, col : col + P].bitcast(E4M3),
+                        lhsT_scale=w2_scales[:, col : col + P],
+                        rhs=g_codes[:].bitcast(E5M2),
+                        rhs_scale=g_scales[:],
+                        start=True,
+                        stop=True,
+                    )
+                    nc.vector.scalar_tensor_tensor(da_bf[:, t, :], a_raw[h][:, t, :], 0.0, dh[:], MAX, MULT)
+                da_mix = work.tile([P, C, J], BF16, name="da_mix", align_bytes=64)
+                nc.scalar.activation(
+                    da_mix[:].rearrange("p (c i) t -> p c t i", i=4), da_bf[:].rearrange("p t (c i) -> p c t i", i=4), COPY
+                )
+                codes = work.tile([P, C], U32, name="da_codes", bufs=3, align_bytes=64)
+                scales = work.tile([P, C], U8, name="da_scales", bufs=3, align_bytes=64)
+                nc.vector.quantize_mx(
+                    out=codes[:].bitcast(E5M2), scales=scales[:], in_=da_mix[:].rearrange("p c t -> p (c t)")
+                )
+                da_codes.append((codes, scales))
+
+                nc.scalar.activation(
+                    w1_bf[:, h * K : (h + 1) * K, :].rearrange("p (c i) j -> p c j i", i=4),
+                    w1_raw[h][:].rearrange("p j (c i) -> p c j i", i=4),
+                    COPY,
+                )
+            for lo, hi in ((0, 512), (512, HALVES * K)):
+                nc.vector.quantize_mx(
+                    out=w1_codes[:, lo:hi].bitcast(E4M3),
+                    scales=w1_scales[:, lo:hi],
+                    in_=w1_bf[:, lo:hi, :].rearrange("p c j -> p (c j)"),
+                )
+
+            for k in range(K_TILES):
+                dx = psum.tile([P, C], F32, name="dx", bufs=3)
+                for h in range(HALVES):
+                    col = h * K + k * P
+                    codes, scales = da_codes[h]
+                    nc.tensor.matmul_mx(
+                        out=dx[:],
+                        lhsT=w1_codes[:, col : col + P].bitcast(E4M3),
+                        lhsT_scale=w1_scales[:, col : col + P],
+                        rhs=codes[:].bitcast(E5M2),
+                        rhs_scale=scales[:],
+                        start=(h == 0),
+                        stop=(h == HALVES - 1),
+                    )
+                result = work.tile([P, C], F32, name="result", bufs=9)
+                nc.scalar.activation(result[:], dx[:], COPY, scale=2.0)
+                results.append((e, k, result))
+
+        for e, k, result in results:
+            nc.vector.tensor_copy(windows[k][:].indirect(offsets[:, e * C // 16 : (e + 1) * C // 16]), result[:])
+            if e == E - 1:
+                nc.sync.dma_start(out[k * P : (k + 1) * P, :], windows[k][:])

@@ -35,130 +35,207 @@ def tile_moe_bdx_mlp_relu2_kernel(tc, dyT, a, w2, w1, gate, offs, out):
         tokens = [held.tile([P, T], F32, name=f"tokens{t}") for t in range(J)]
         windows = [held.tile([P, T], F32, name=f"window{k}") for k in range(K_TILES)]
 
+        dy_rows = dyT.rearrange("(p t) s -> p t s", t=J)
+        a_rows = a.rearrange("(h p t) s -> h p t s", p=P, t=J)
+        w2_raw, a_raw, w1_raw, gathered, g_mx, w2_mx, w1_mx, da_mx, dx_banks, results = {}, {}, {}, {}, {}, {}, {}, {}, {}, {}
+
+        def listed(e):
+            return offsets[:, e * C // 16 : (e + 1) * C // 16]
+
+        def load_tokens(t):
+            nc.sync.dma_start(tokens[t][:], dy_rows[:, t, :])
+
         def load_gate(e):
             nc.sync.dma_start(gates[e][:], gate[0:P, e * C : (e + 1) * C])
 
-        dy_rows = dyT.rearrange("(p t) s -> p t s", t=J)
-        load_gate(0)
-        nc.sync.dma_start(tokens[0][:], dy_rows[:, 0, :])
-        load_gate(1)
-        for t in range(1, J):
-            nc.sync.dma_start(tokens[t][:], dy_rows[:, t, :])
-
-        a_rows = a.rearrange("(h p t) s -> h p t s", p=P, t=J)
-        results = []
-        for e in range(E):
-            slots = slice(e * C, (e + 1) * C)
-            w2_rows = w2[e].rearrange("(p j) i -> p j i", j=J)
-            w1_rows = w1[e].rearrange("(h p j) k -> h p j k", p=P, j=J)
-
-            w2_raw = []
+        def load_w2(e):
+            rows = w2[e].rearrange("(p j) i -> p j i", j=J)
             for h in range(HALVES):
                 raw = work.tile([P, J, P * J], F32, name="w2_raw", bufs=3)
-                nc.sync.dma_start(raw[:], w2_rows[:, :, h * P * J : (h + 1) * P * J])
-                w2_raw.append(raw)
-            if e == 0:
-                load_gate(2)
-                load_gate(3)
-            a_raw = []
-            for h in range(HALVES):
-                raw = work.tile([P, J, C], F32, name="a_raw", bufs=3)
-                nc.sync.dma_start(raw[:], a_rows[h][:, :, slots])
-                a_raw.append(raw)
-            w1_raw = []
-            for h in range(HALVES):
-                raw = work.tile([P, J, K], F32, name="w1_raw", bufs=2)
-                nc.sync.dma_start(raw[:], w1_rows[h])
-                w1_raw.append(raw)
+                nc.sync.dma_start(raw[:], rows[:, :, h * P * J : (h + 1) * P * J])
+                w2_raw[e, h] = raw
 
-            gathered = work.tile([P, J, C], F32, name="gathered")
+        def load_a(e):
+            for h in range(HALVES):
+                raw = work.tile([P, J, C], F32, name="a_raw", bufs=4)
+                nc.sync.dma_start(raw[:], a_rows[h][:, :, e * C : (e + 1) * C])
+                a_raw[e, h] = raw
+
+        def load_w1(e):
+            rows = w1[e].rearrange("(h p j) k -> h p j k", p=P, j=J)
+            for h in range(HALVES):
+                raw = work.tile([P, J, K], F32, name="w1_raw", bufs=3)
+                nc.sync.dma_start(raw[:], rows[h])
+                w1_raw[e, h] = raw
+
+        def gather(e):
+            gathered[e] = work.tile([P, J, C], F32, name="gathered", bufs=2)
             for t in range(J):
-                nc.vector.tensor_tensor(
-                    gathered[:, t, :], tokens[t][:].indirect(offsets[:, e * C // 16 : (e + 1) * C // 16]), gates[e][:], MULT
-                )
-            g_bf = work.tile([P, C, J], BF16, name="g_bf", align_bytes=64)
-            nc.scalar.activation(
-                g_bf[:].rearrange("p (c i) t -> p c t i", i=4), gathered[:].rearrange("p t (c i) -> p c t i", i=4), COPY
-            )
-            g_codes = work.tile([P, C], U32, name="g_codes", align_bytes=64)
-            g_scales = work.tile([P, C], U8, name="g_scales", align_bytes=64)
-            nc.vector.quantize_mx(
-                out=g_codes[:].bitcast(E5M2), scales=g_scales[:], in_=g_bf[:].rearrange("p c t -> p (c t)")
-            )
+                nc.vector.tensor_tensor(gathered[e][:, t, :], tokens[t][:].indirect(listed(e)), gates[e][:], MULT)
 
-            w2_codes = work.tile([P, H], U32, name="w2_codes", align_bytes=64)
-            w2_scales = work.tile([P, H], U8, name="w2_scales", align_bytes=64)
+        def quantize_g(e):
+            mixed = work.tile([P, C, J], BF16, name="g_mixed", align_bytes=64)
+            nc.scalar.activation(
+                mixed[:].rearrange("p (c i) t -> p c t i", i=4), gathered[e][:].rearrange("p t (c i) -> p c t i", i=4), COPY
+            )
+            codes = work.tile([P, C], U32, name="g_codes", bufs=3, align_bytes=64)
+            scales = work.tile([P, C], U8, name="g_scales", bufs=3, align_bytes=64)
+            nc.vector.quantize_mx(out=codes[:].bitcast(E5M2), scales=scales[:], in_=mixed[:].rearrange("p c t -> p (c t)"))
+            g_mx[e] = codes, scales
+
+        def quantize_w2(e):
+            codes = work.tile([P, H], U32, name="w2_codes", align_bytes=64)
+            scales = work.tile([P, H], U8, name="w2_scales", align_bytes=64)
             for h in range(HALVES):
-                w2_bf = work.tile([P, J, P, J], BF16, name="w2_bf", align_bytes=64)
+                mixed = work.tile([P, J, P, J], BF16, name="w2_mixed", bufs=2, align_bytes=64)
                 nc.scalar.activation(
-                    w2_bf[:].rearrange("p t m j -> p m t j"), w2_raw[h][:].rearrange("p j (m t) -> p m t j", t=J), COPY
+                    mixed[:].rearrange("p t m j -> p m t j"), w2_raw[e, h][:].rearrange("p j (m t) -> p m t j", t=J), COPY
                 )
                 cols = slice(h * P * J, (h + 1) * P * J)
                 nc.vector.quantize_mx(
-                    out=w2_codes[:, cols].bitcast(E4M3), scales=w2_scales[:, cols], in_=w2_bf[:].rearrange("p t m j -> p (t m j)")
+                    out=codes[:, cols].bitcast(E4M3), scales=scales[:, cols], in_=mixed[:].rearrange("p t m j -> p (t m j)")
                 )
+            w2_mx[e] = codes, scales
 
-            w1_bf = work.tile([P, HALVES * K, J], BF16, name="w1_bf", align_bytes=64)
-            w1_codes = work.tile([P, HALVES * K], U32, name="w1_codes", align_bytes=64)
-            w1_scales = work.tile([P, HALVES * K], U8, name="w1_scales", align_bytes=64)
-            da_codes = []
+        def quantize_w1(e):
+            mixed = work.tile([P, HALVES * K, J], BF16, name="w1_mixed", bufs=2, align_bytes=64)
+            codes = work.tile([P, HALVES * K], U32, name="w1_codes", align_bytes=64)
+            scales = work.tile([P, HALVES * K], U8, name="w1_scales", align_bytes=64)
             for h in range(HALVES):
-                da_bf = work.tile([P, J, C], BF16, name="da_bf")
-                for t in range(J):
-                    dh = psum.tile([P, C], F32, name="dh", bufs=5)
-                    col = (h * J + t) * P
-                    nc.tensor.matmul_mx(
-                        out=dh[:],
-                        lhsT=w2_codes[:, col : col + P].bitcast(E4M3),
-                        lhsT_scale=w2_scales[:, col : col + P],
-                        rhs=g_codes[:].bitcast(E5M2),
-                        rhs_scale=g_scales[:],
-                        start=True,
-                        stop=True,
-                    )
-                    nc.vector.scalar_tensor_tensor(da_bf[:, t, :], a_raw[h][:, t, :], 0.0, dh[:], MAX, MULT)
-                da_mix = work.tile([P, C, J], BF16, name="da_mix", align_bytes=64)
                 nc.scalar.activation(
-                    da_mix[:].rearrange("p (c i) t -> p c t i", i=4), da_bf[:].rearrange("p t (c i) -> p c t i", i=4), COPY
-                )
-                codes = work.tile([P, C], U32, name="da_codes", bufs=3, align_bytes=64)
-                scales = work.tile([P, C], U8, name="da_scales", bufs=3, align_bytes=64)
-                nc.vector.quantize_mx(
-                    out=codes[:].bitcast(E5M2), scales=scales[:], in_=da_mix[:].rearrange("p c t -> p (c t)")
-                )
-                da_codes.append((codes, scales))
-
-                nc.scalar.activation(
-                    w1_bf[:, h * K : (h + 1) * K, :].rearrange("p (c i) j -> p c j i", i=4),
-                    w1_raw[h][:].rearrange("p j (c i) -> p c j i", i=4),
+                    mixed[:, h * K : (h + 1) * K, :].rearrange("p (c i) j -> p c j i", i=4),
+                    w1_raw[e, h][:].rearrange("p j (c i) -> p c j i", i=4),
                     COPY,
                 )
             for lo, hi in ((0, 512), (512, HALVES * K)):
                 nc.vector.quantize_mx(
-                    out=w1_codes[:, lo:hi].bitcast(E4M3),
-                    scales=w1_scales[:, lo:hi],
-                    in_=w1_bf[:, lo:hi, :].rearrange("p c j -> p (c j)"),
+                    out=codes[:, lo:hi].bitcast(E4M3),
+                    scales=scales[:, lo:hi],
+                    in_=mixed[:, lo:hi, :].rearrange("p c j -> p (c j)"),
                 )
+            w1_mx[e] = codes, scales
 
+        def hidden_gradient(e, h):
+            w2_codes, w2_scales = w2_mx[e]
+            g_codes, g_scales = g_mx[e]
+            da = work.tile([P, J, C], BF16, name="da")
+            for t in range(J):
+                dh = psum.tile([P, C], F32, name="dh", bufs=5)
+                col = (h * J + t) * P
+                nc.tensor.matmul_mx(
+                    out=dh[:],
+                    lhsT=w2_codes[:, col : col + P].bitcast(E4M3),
+                    lhsT_scale=w2_scales[:, col : col + P],
+                    rhs=g_codes[:].bitcast(E5M2),
+                    rhs_scale=g_scales[:],
+                    start=True,
+                    stop=True,
+                )
+                nc.vector.scalar_tensor_tensor(da[:, t, :], a_raw[e, h][:, t, :], 0.0, dh[:], MAX, MULT)
+            mixed = work.tile([P, C, J], BF16, name="da_mixed", align_bytes=64)
+            nc.scalar.activation(mixed[:].rearrange("p (c i) t -> p c t i", i=4), da[:].rearrange("p t (c i) -> p c t i", i=4), COPY)
+            codes = work.tile([P, C], U32, name="da_codes", bufs=3, align_bytes=64)
+            scales = work.tile([P, C], U8, name="da_scales", bufs=3, align_bytes=64)
+            nc.vector.quantize_mx(out=codes[:].bitcast(E5M2), scales=scales[:], in_=mixed[:].rearrange("p c t -> p (c t)"))
+            da_mx[e, h] = codes, scales
+
+        def input_gradient(e):
+            w1_codes, w1_scales = w1_mx[e]
             for k in range(K_TILES):
                 dx = psum.tile([P, C], F32, name="dx", bufs=3)
                 for h in range(HALVES):
                     col = h * K + k * P
-                    codes, scales = da_codes[h]
+                    da_codes, da_scales = da_mx[e, h]
                     nc.tensor.matmul_mx(
                         out=dx[:],
                         lhsT=w1_codes[:, col : col + P].bitcast(E4M3),
                         lhsT_scale=w1_scales[:, col : col + P],
-                        rhs=codes[:].bitcast(E5M2),
-                        rhs_scale=scales[:],
+                        rhs=da_codes[:].bitcast(E5M2),
+                        rhs_scale=da_scales[:],
                         start=(h == 0),
                         stop=(h == HALVES - 1),
                     )
-                result = work.tile([P, C], F32, name="result", bufs=9)
-                nc.scalar.activation(result[:], dx[:], COPY, scale=2.0)
-                results.append((e, k, result))
+                dx_banks[e, k] = dx
 
-        for e, k, result in results:
-            nc.vector.tensor_copy(windows[k][:].indirect(offsets[:, e * C // 16 : (e + 1) * C // 16]), result[:])
+        def copy_out(e, k, h):
+            plane = a_raw[min(e + 1, E - 1), h][:, k, :]
+            nc.scalar.activation(plane, dx_banks[e, k][:], COPY, scale=2.0)
+            results[e, k] = plane
+
+        def scatter(e, k):
+            nc.vector.tensor_copy(windows[k][:].indirect(listed(e)), results[e, k])
             if e == E - 1:
                 nc.sync.dma_start(out[k * P : (k + 1) * P, :], windows[k][:])
+
+        load_gate(0)
+        load_tokens(0)
+        load_gate(1)
+        load_tokens(1)
+        load_tokens(2)
+        load_tokens(3)
+        load_w2(0)
+        load_gate(2)
+        load_gate(3)
+        load_a(0)
+        load_w1(0)
+        load_w2(1)
+        load_a(1)
+        load_w1(1)
+        load_w2(2)
+        load_a(2)
+        load_w1(2)
+        load_w2(3)
+        load_a(3)
+        load_w1(3)
+        gather(0)
+        quantize_g(0)
+        gather(1)
+        quantize_w2(0)
+        hidden_gradient(0, 0)
+        quantize_w1(0)
+        quantize_g(1)
+        quantize_w2(1)
+        hidden_gradient(0, 1)
+        input_gradient(0)
+        gather(2)
+        hidden_gradient(1, 0)
+        copy_out(0, 2, 0)
+        copy_out(0, 0, 0)
+        quantize_w1(1)
+        quantize_g(2)
+        quantize_w2(2)
+        scatter(0, 0)
+        hidden_gradient(1, 1)
+        copy_out(0, 1, 0)
+        input_gradient(1)
+        gather(3)
+        hidden_gradient(2, 0)
+        copy_out(1, 2, 0)
+        copy_out(1, 0, 0)
+        quantize_w1(2)
+        quantize_g(3)
+        scatter(0, 1)
+        quantize_w2(3)
+        scatter(1, 0)
+        hidden_gradient(2, 1)
+        scatter(0, 2)
+        copy_out(1, 1, 0)
+        input_gradient(2)
+        hidden_gradient(3, 0)
+        copy_out(2, 2, 0)
+        copy_out(2, 0, 0)
+        quantize_w1(3)
+        scatter(1, 1)
+        scatter(2, 0)
+        hidden_gradient(3, 1)
+        scatter(1, 2)
+        copy_out(2, 1, 0)
+        input_gradient(3)
+        copy_out(3, 0, 1)
+        copy_out(3, 1, 1)
+        copy_out(3, 2, 1)
+        scatter(2, 1)
+        scatter(2, 2)
+        scatter(3, 0)
+        scatter(3, 1)
+        scatter(3, 2)

@@ -48,25 +48,19 @@ def tile_moe_bdx_mlp_relu2_kernel(tc, dyT, a, w2, w1, gate, offs, out):
         def load_gate(e):
             nc.sync.dma_start(gates[e][:], gate[0:P, e * C : (e + 1) * C])
 
-        def load_w2(e):
+        def load_w2(e, h):
+            w2_raw[e, h] = work.tile([P, J, P * J], F32, name="w2_raw", bufs=3)
             rows = w2[e].rearrange("(p j) i -> p j i", j=J)
-            for h in range(HALVES):
-                raw = work.tile([P, J, P * J], F32, name="w2_raw", bufs=3)
-                nc.sync.dma_start(raw[:], rows[:, :, h * P * J : (h + 1) * P * J])
-                w2_raw[e, h] = raw
+            nc.sync.dma_start(w2_raw[e, h][:], rows[:, :, h * P * J : (h + 1) * P * J])
 
-        def load_a(e):
-            for h in range(HALVES):
-                raw = work.tile([P, J, C], F32, name="a_raw", bufs=4)
-                nc.sync.dma_start(raw[:], a_rows[h][:, :, e * C : (e + 1) * C])
-                a_raw[e, h] = raw
+        def load_a(e, h):
+            a_raw[e, h] = work.tile([P, J, C], F32, name="a_raw", bufs=4)
+            nc.sync.dma_start(a_raw[e, h][:], a_rows[h][:, :, e * C : (e + 1) * C])
 
-        def load_w1(e):
-            rows = w1[e].rearrange("(h p j) k -> h p j k", p=P, j=J)
-            for h in range(HALVES):
-                raw = work.tile([P, J, K], F32, name="w1_raw", bufs=3)
-                nc.sync.dma_start(raw[:], rows[h])
-                w1_raw[e, h] = raw
+        def load_w1(e, h):
+            w1_raw[e, h] = work.tile([P, J, K], F32, name="w1_raw", bufs=3)
+            nc.sync.dma_start(w1_raw[e, h][:], w1[e].rearrange("(h p j) k -> h p j k", p=P, j=J)[h])
+
 
         def gather(e):
             gathered[e] = work.tile([P, J, C], F32, name="gathered", bufs=2)
@@ -89,7 +83,7 @@ def tile_moe_bdx_mlp_relu2_kernel(tc, dyT, a, w2, w1, gate, offs, out):
             for h in range(HALVES):
                 mixed = work.tile([P, J, P, J], BF16, name="w2_mixed", bufs=2, align_bytes=64)
                 nc.scalar.activation(
-                    mixed[:].rearrange("p t m j -> p m t j"), w2_raw[e, h][:].rearrange("p j (m t) -> p m t j", t=J), COPY
+                    mixed[:].rearrange("p t m j -> p m j t"), w2_raw[e, h][:].rearrange("p j (m t) -> p m j t", t=J), COPY
                 )
                 cols = slice(h * P * J, (h + 1) * P * J)
                 nc.vector.quantize_mx(
@@ -133,7 +127,7 @@ def tile_moe_bdx_mlp_relu2_kernel(tc, dyT, a, w2, w1, gate, offs, out):
                 )
                 nc.vector.scalar_tensor_tensor(da[:, t, :], a_raw[e, h][:, t, :], 0.0, dh[:], MAX, MULT)
             mixed = work.tile([P, C, J], BF16, name="da_mixed", align_bytes=64)
-            nc.scalar.activation(mixed[:].rearrange("p (c i) t -> p c t i", i=4), da[:].rearrange("p t (c i) -> p c t i", i=4), COPY)
+            nc.scalar.activation(mixed[:].rearrange("p (c i) t -> p c t i", i=8), da[:].rearrange("p t (c i) -> p c t i", i=8), COPY)
             codes = work.tile([P, C], U32, name="da_codes", bufs=3, align_bytes=64)
             scales = work.tile([P, C], U8, name="da_scales", bufs=3, align_bytes=64)
             nc.vector.quantize_mx(out=codes[:].bitcast(E5M2), scales=scales[:], in_=mixed[:].rearrange("p c t -> p (c t)"))
@@ -173,20 +167,32 @@ def tile_moe_bdx_mlp_relu2_kernel(tc, dyT, a, w2, w1, gate, offs, out):
         load_tokens(1)
         load_tokens(2)
         load_tokens(3)
-        load_w2(0)
+        load_w2(0, 0)
+        load_w2(0, 1)
         load_gate(2)
         load_gate(3)
-        load_a(0)
-        load_w1(0)
-        load_w2(1)
-        load_a(1)
-        load_w1(1)
-        load_w2(2)
-        load_a(2)
-        load_w1(2)
-        load_w2(3)
-        load_a(3)
-        load_w1(3)
+        load_a(0, 0)
+        load_a(0, 1)
+        load_w1(0, 0)
+        load_w1(0, 1)
+        load_w2(1, 0)
+        load_w2(1, 1)
+        load_a(1, 0)
+        load_a(1, 1)
+        load_w1(1, 0)
+        load_w1(1, 1)
+        load_w2(2, 0)
+        load_w2(2, 1)
+        load_a(2, 0)
+        load_a(2, 1)
+        load_w1(2, 0)
+        load_w1(2, 1)
+        load_w2(3, 0)
+        load_w2(3, 1)
+        load_a(3, 0)
+        load_a(3, 1)
+        load_w1(3, 0)
+        load_w1(3, 1)
         gather(0)
         quantize_g(0)
         gather(1)

from contextlib import ExitStack

import concourse.mybir as mybir

K, T, E, C, H, N = 384, 2048, 4, 512, 1024, 512
P = 128
J = 4
HALVES = H // (P * J)
K_TILES = K // P
FLOPS = 2 * E * C * (N * H + H * K)
BYTES = 4 * (N * T + H * E * C + E * N * H + E * H * K + E * C + K * T) + 2 * P * (E * C // 16)

F32 = mybir.dt.float32
BF16 = mybir.dt.bfloat16
U32 = mybir.dt.uint32
U16 = mybir.dt.uint16
U8 = mybir.dt.uint8
E4M3 = mybir.dt.float8_e4m3fn_x4
E5M2 = mybir.dt.float8_e5m2_x4
MULT = mybir.AluOpType.mult
MAX = mybir.AluOpType.max
COPY = mybir.ActivationFunctionType.Copy


def tile_moe_bdx_mlp_relu2_kernel(tc, dyT, a, w2, w1, gate, offs, out):
    nc = tc.nc
    with ExitStack() as ctx:
        held = ctx.enter_context(tc.tile_pool(name="held", bufs=1))
        work = ctx.enter_context(tc.tile_pool(name="work", bufs=2))
        psum = ctx.enter_context(tc.psum_pool(name="psum", bufs=1))

        offsets = held.tile([P, E * C // 16], U16, name="offsets")
        nc.sync.dma_start(offsets[:], offs)
        gates = [held.tile([P, C], F32, name=f"gate{e}") for e in range(E)]
        tokens = [held.tile([P, T], F32, name=f"tokens{t}") for t in range(J)]
        windows = [held.tile([P, T], F32, name=f"window{k}") for k in range(K_TILES)]

        dy_rows = dyT.rearrange("(p t) s -> p t s", t=J)
        a_rows = a.rearrange("(h p t) s -> h p t s", p=P, t=J)
        w2_raw, a_raw, w1_raw, gathered, g_mx, w2_mx, w1_mx, da_mx, dx_banks, results = {}, {}, {}, {}, {}, {}, {}, {}, {}, {}

        def listed(e):
            return offsets[:, e * C // 16 : (e + 1) * C // 16]

        def load_tokens(t):
            nc.sync.dma_start(tokens[t][:], dy_rows[:, t, :])

        def load_gate(e):
            nc.sync.dma_start(gates[e][:], gate[0:P, e * C : (e + 1) * C])

        def load_w2(e, h):
            w2_raw[e, h] = work.tile([P, J, P * J], F32, name="w2_raw", bufs=3)
            rows = w2[e].rearrange("(p j) i -> p j i", j=J)
            nc.sync.dma_start(w2_raw[e, h][:], rows[:, :, h * P * J : (h + 1) * P * J])

        def load_a(e, h):
            a_raw[e, h] = work.tile([P, J, C], F32, name="a_raw", bufs=4)
            nc.sync.dma_start(a_raw[e, h][:], a_rows[h][:, :, e * C : (e + 1) * C])

        def load_w1(e, h):
            w1_raw[e, h] = work.tile([P, J, K], F32, name="w1_raw", bufs=3)
            nc.sync.dma_start(w1_raw[e, h][:], w1[e].rearrange("(h p j) k -> h p j k", p=P, j=J)[h])


        def gather(e):
            gathered[e] = work.tile([P, J, C], F32, name="gathered", bufs=2)
            for t in range(J):
                nc.vector.tensor_tensor(gathered[e][:, t, :], tokens[t][:].indirect(listed(e)), gates[e][:], MULT)

        def quantize_g(e):
            mixed = work.tile([P, C, J], BF16, name="g_mixed", align_bytes=64)
            nc.scalar.activation(
                mixed[:].rearrange("p (c i) t -> p c t i", i=4), gathered[e][:].rearrange("p t (c i) -> p c t i", i=4), COPY
            )
            codes = work.tile([P, C], U32, name="g_codes", bufs=3, align_bytes=64)
            scales = work.tile([P, C], U8, name="g_scales", bufs=3, align_bytes=64)
            nc.vector.quantize_mx(out=codes[:].bitcast(E5M2), scales=scales[:], in_=mixed[:].rearrange("p c t -> p (c t)"))
            g_mx[e] = codes, scales

        def quantize_w2(e):
            codes = work.tile([P, H], U32, name="w2_codes", align_bytes=64)
            scales = work.tile([P, H], U8, name="w2_scales", align_bytes=64)
            for h in range(HALVES):
                mixed = work.tile([P, J, P, J], BF16, name="w2_mixed", bufs=2, align_bytes=64)
                nc.scalar.activation(
                    mixed[:].rearrange("p t m j -> p m j t"), w2_raw[e, h][:].rearrange("p j (m t) -> p m j t", t=J), COPY
                )
                cols = slice(h * P * J, (h + 1) * P * J)
                nc.vector.quantize_mx(
                    out=codes[:, cols].bitcast(E4M3), scales=scales[:, cols], in_=mixed[:].rearrange("p t m j -> p (t m j)")
                )
            w2_mx[e] = codes, scales

        def quantize_w1(e):
            mixed = work.tile([P, HALVES * K, J], BF16, name="w1_mixed", bufs=2, align_bytes=64)
            codes = work.tile([P, HALVES * K], U32, name="w1_codes", align_bytes=64)
            scales = work.tile([P, HALVES * K], U8, name="w1_scales", align_bytes=64)
            for h in range(HALVES):
                nc.scalar.activation(
                    mixed[:, h * K : (h + 1) * K, :].rearrange("p (c i) j -> p c j i", i=4),
                    w1_raw[e, h][:].rearrange("p j (c i) -> p c j i", i=4),
                    COPY,
                )
            for lo, hi in ((0, 512), (512, HALVES * K)):
                nc.vector.quantize_mx(
                    out=codes[:, lo:hi].bitcast(E4M3),
                    scales=scales[:, lo:hi],
                    in_=mixed[:, lo:hi, :].rearrange("p c j -> p (c j)"),
                )
            w1_mx[e] = codes, scales

        def hidden_gradient(e, h):
            w2_codes, w2_scales = w2_mx[e]
            g_codes, g_scales = g_mx[e]
            da = work.tile([P, J, C], BF16, name="da")
            for t in range(J):
                dh = psum.tile([P, C], F32, name="dh", bufs=5)
                col = (h * J + t) * P
                nc.tensor.matmul_mx(
                    out=dh[:],
                    lhsT=w2_codes[:, col : col + P].bitcast(E4M3),
                    lhsT_scale=w2_scales[:, col : col + P],
                    rhs=g_codes[:].bitcast(E5M2),
                    rhs_scale=g_scales[:],
                    start=True,
                    stop=True,
                )
                nc.vector.scalar_tensor_tensor(da[:, t, :], a_raw[e, h][:, t, :], 0.0, dh[:], MAX, MULT)
            mixed = work.tile([P, C, J], BF16, name="da_mixed", align_bytes=64)
            nc.scalar.activation(mixed[:].rearrange("p (c i) t -> p c t i", i=8), da[:].rearrange("p t (c i) -> p c t i", i=8), COPY)
            codes = work.tile([P, C], U32, name="da_codes", bufs=3, align_bytes=64)
            scales = work.tile([P, C], U8, name="da_scales", bufs=3, align_bytes=64)
            nc.vector.quantize_mx(out=codes[:].bitcast(E5M2), scales=scales[:], in_=mixed[:].rearrange("p c t -> p (c t)"))
            da_mx[e, h] = codes, scales

        def input_gradient(e):
            w1_codes, w1_scales = w1_mx[e]
            for k in range(K_TILES):
                dx = psum.tile([P, C], F32, name="dx", bufs=3)
                for h in range(HALVES):
                    col = h * K + k * P
                    da_codes, da_scales = da_mx[e, h]
                    nc.tensor.matmul_mx(
                        out=dx[:],
                        lhsT=w1_codes[:, col : col + P].bitcast(E4M3),
                        lhsT_scale=w1_scales[:, col : col + P],
                        rhs=da_codes[:].bitcast(E5M2),
                        rhs_scale=da_scales[:],
                        start=(h == 0),
                        stop=(h == HALVES - 1),
                    )
                dx_banks[e, k] = dx

        def copy_out(e, k, h):
            plane = a_raw[min(e + 1, E - 1), h][:, k, :]
            nc.scalar.activation(plane, dx_banks[e, k][:], COPY, scale=2.0)
            results[e, k] = plane

        def scatter(e, k):
            nc.vector.tensor_copy(windows[k][:].indirect(listed(e)), results[e, k])
            if e == E - 1:
                nc.sync.dma_start(out[k * P : (k + 1) * P, :], windows[k][:])

        load_gate(0)
        load_tokens(0)
        load_gate(1)
        load_tokens(1)
        load_tokens(2)
        load_tokens(3)
        load_w2(0, 0)
        load_w2(0, 1)
        load_gate(2)
        load_gate(3)
        load_a(0, 0)
        load_a(0, 1)
        load_w1(0, 0)
        load_w1(0, 1)
        load_w2(1, 0)
        load_w2(1, 1)
        load_a(1, 0)
        load_a(1, 1)
        load_w1(1, 0)
        load_w1(1, 1)
        load_w2(2, 0)
        load_w2(2, 1)
        load_a(2, 0)
        load_a(2, 1)
        load_w1(2, 0)
        load_w1(2, 1)
        load_w2(3, 0)
        load_w2(3, 1)
        load_a(3, 0)
        load_a(3, 1)
        load_w1(3, 0)
        load_w1(3, 1)
        gather(0)
        quantize_g(0)
        gather(1)
        quantize_w2(0)
        hidden_gradient(0, 0)
        quantize_w1(0)
        quantize_g(1)
        quantize_w2(1)
        hidden_gradient(0, 1)
        input_gradient(0)
        gather(2)
        hidden_gradient(1, 0)
        copy_out(0, 2, 0)
        copy_out(0, 0, 0)
        quantize_w1(1)
        quantize_g(2)
        quantize_w2(2)
        scatter(0, 0)
        hidden_gradient(1, 1)
        copy_out(0, 1, 0)
        input_gradient(1)
        gather(3)
        hidden_gradient(2, 0)
        copy_out(1, 2, 0)
        copy_out(1, 0, 0)
        quantize_w1(2)
        quantize_g(3)
        scatter(0, 1)
        quantize_w2(3)
        scatter(1, 0)
        hidden_gradient(2, 1)
        scatter(0, 2)
        copy_out(1, 1, 0)
        input_gradient(2)
        hidden_gradient(3, 0)
        copy_out(2, 2, 0)
        copy_out(2, 0, 0)
        quantize_w1(3)
        scatter(1, 1)
        scatter(2, 0)
        hidden_gradient(3, 1)
        scatter(1, 2)
        copy_out(2, 1, 0)
        input_gradient(3)
        copy_out(3, 0, 1)
        copy_out(3, 1, 1)
        copy_out(3, 2, 1)
        scatter(2, 1)
        scatter(2, 2)
        scatter(3, 0)
        scatter(3, 1)
        scatter(3, 2)
